import numpy as np
import ml_dtypes


def mxq(x, axis, fmt="e4m3"):
    dtype, down = {"e4m3": (ml_dtypes.float8_e4m3fn, 7), "e5m2": (ml_dtypes.float8_e5m2, 14)}[fmt]
    v = np.moveaxis(np.asarray(x, np.float32).astype(ml_dtypes.bfloat16).astype(np.float64), axis, -1)
    blocks = v.reshape(v.shape[:-1] + (-1, 32))
    amax = np.abs(blocks).max(-1, keepdims=True)
    byte = np.maximum(np.where(amax > 0, np.frexp(amax)[1] - 1 + 127, 0) - down, 1)
    scale = np.exp2(byte - 127.0)
    codes = (blocks / scale).astype(np.float32).astype(dtype).astype(np.float64)
    return np.moveaxis((codes * scale).reshape(v.shape), -1, axis)


WIDE = False


def mx_kscale(k):
    if not WIDE:
        return np.ones(k)
    levels = np.array([10, -10, 5, -5, 0])
    if k % 512:
        return np.exp2(np.random.permutation(np.resize(levels, k // 32))).repeat(32)
    a = np.empty((k // 512, 16))
    for p in range(k // 512):
        a[p, :8] = np.random.permutation(np.resize(levels, 8))
        for g in range(8):
            far = levels[np.abs(levels - a[p, g]) >= 10]
            a[p, g + 8] = far[np.random.randint(len(far))]
    return np.exp2(a.ravel()).repeat(32)


def f64(x):
    return np.asarray(x).astype(np.float64)


def striped(idx):
    return np.tile(idx.reshape(-1, 16).T, (8, 1)).astype(np.uint16)


def unstriped(offs):
    return offs[:16].T.reshape(-1).astype(np.int64)


K, T, D, S, V, N = 512, 2048, 16, 1024, 64, 512


def setup_inputs():
    n = np.random.standard_normal
    s = mx_kscale(K)[:, None]
    return {
        "xT": (n((K, T)) * s).astype(np.float32),
        "w": (n((K, N)) / np.sqrt(K) / s).astype(np.float32),
        "b": (0.3 * n((N, 1))).astype(np.float32),
        "offs": striped(np.random.permutation(T)[:S]),
    }


def reference(xT, w, b, offs):
    idx = unstriped(offs)
    xq = mxq(f64(xT)[:, idx], 0, "e4m3")
    y = mxq(f64(w), 0, "e4m3").T @ xq
    y = y + f64(b)
    return y.reshape(N, V, D).max(axis=2)

@@ -1,0 +1,174 @@
+from contextlib import ExitStack
+
+import concourse.mybir as mybir
+
+K, T, D, S, V, N = 512, 2048, 16, 1024, 64, 512
+FLOPS = 2 * K * N * S
+
+F32 = mybir.dt.float32
+BF16 = mybir.dt.bfloat16
+U32 = mybir.dt.uint32
+U16 = mybir.dt.uint16
+U8 = mybir.dt.uint8
+FP8X4 = mybir.dt.float8_e4m3fn_x4
+COPY = mybir.ActivationFunctionType.Copy
+IDENTITY = mybir.ActivationFunctionType.Identity
+
+P = 128
+PACK = 4
+SLICE = 256
+SLICES = S // SLICE
+HALF = 256
+ROW2_CUTS = [0, 1024, 2048]
+PAIR_CUTS = [0, 1024, 1536, 2048]
+PAIR_LAST_SPLIT = 1856
+ROW3_CUTS = [0, 512, 1024, 1536, 2048]
+
+
+def spans(cuts):
+    return [slice(a, c) for a, c in zip(cuts[:-1], cuts[1:])]
+
+
+def tile_picked_pool_lin_bias_sub_e_kernel(tc, xT, w, b, offs, out):
+    nc = tc.nc
+    xv = xT.rearrange("(p j) t -> p j t", j=PACK)
+    wv = w.rearrange("(p j) m -> p j m", j=PACK)
+
+    with ExitStack() as ctx:
+        keep = ctx.enter_context(tc.tile_pool(name="keep", bufs=1))
+        psum = ctx.enter_context(tc.psum_pool(name="psum", bufs=1))
+
+        offsets = keep.tile([P, S // 16], U16, name="offsets")
+        raw01 = keep.tile([P, 2, T], F32, name="raw01")
+        raw2 = keep.tile([P, T], F32, name="raw2")
+        raw3 = keep.tile([P, T], F32, name="raw3")
+        pairs = keep.tile([P, T, 2], BF16, name="pairs")
+        row2 = keep.tile([P, T], BF16, name="row2")
+        row3 = keep.tile([P, T], BF16, name="row3")
+        picked = [keep.tile([P, SLICE, PACK], BF16, name="picked%d" % s, align_bytes=64) for s in range(SLICES)]
+        x_codes = keep.tile([P, S], U32, name="x_codes", align_bytes=64)
+        x_scales = keep.tile([P, S], U8, name="x_scales", align_bytes=64)
+        w_raw = [keep.tile([P, PACK, HALF], F32, name="w_raw%d" % h) for h in range(2)]
+        w_bf = [keep.tile([P, HALF, PACK], BF16, name="w_bf%d" % h, align_bytes=64) for h in range(2)]
+        w_codes = [keep.tile([P, HALF], U32, name="w_codes%d" % h, align_bytes=64) for h in range(2)]
+        w_scales = [keep.tile([P, HALF], U8, name="w_scales%d" % h, align_bytes=64) for h in range(2)]
+        bias = keep.tile([P, N // P], F32, name="bias")
+        pooled01 = keep.tile([P, 2, V], F32, name="pooled01")
+        result01 = keep.tile([P, 2, V], F32, name="result01")
+        pooled2 = keep.tile([P, V], F32, name="pooled2")
+        result2 = keep.tile([P, V], F32, name="result2")
+        biased3 = keep.tile([P, S], F32, name="biased3")
+        result3 = keep.tile([P, V], F32, name="result3")
+        warm_in = keep.tile([P, 1], F32, name="warm_in")
+        warm_out = keep.tile([P, 1], F32, name="warm_out")
+        banks = [psum.tile([P, 2 * SLICE], F32, name="bank%d" % i) for i in range(8)]
+
+        def listed(s):
+            return offsets[:, s * (SLICE // 16) : (s + 1) * (SLICE // 16)]
+
+        nc.gpsimd.memset(warm_in[:], 0.0)
+        nc.scalar.activation(out=warm_out[:], in_=warm_in[:], func=COPY)
+
+        first, second = spans(ROW2_CUTS)
+        nc.sync.dma_start(out=raw2[:, first], in_=xv[:, 2, first])
+        nc.sync.dma_start(offsets[:], offs)
+        nc.sync.dma_start(out=raw2[:, second], in_=xv[:, 2, second])
+        for c in spans(PAIR_CUTS):
+            nc.sync.dma_start(out=raw01[:, :, c], in_=xv[:, 0:2, c])
+        for c in spans(ROW3_CUTS):
+            nc.sync.dma_start(out=raw3[:, c], in_=xv[:, 3, c])
+        for h in range(2):
+            nc.sync.dma_start(out=w_raw[h][:], in_=wv[:, :, h * HALF : (h + 1) * HALF])
+        with nc.allow_non_contiguous_dma(reason="one bias value a partition"):
+            nc.sync.dma_start(out=bias[:], in_=b.rearrange("(t p) o -> p (t o)", p=P))
+
+        for c in spans(ROW2_CUTS):
+            nc.vector.tensor_copy(out=row2[:, c], in_=raw2[:, c])
+        for s in range(SLICES):
+            nc.scalar.activation(out=picked[s][:, :, 2], in_=row2[:].indirect(listed(s)), func=COPY)
+
+        for c in spans(PAIR_CUTS[:-1] + [PAIR_LAST_SPLIT]):
+            nc.vector.tensor_copy(out=pairs[:, c, :], in_=raw01[:, :, c].rearrange("p j t -> p t j"))
+        c = slice(PAIR_LAST_SPLIT, T)
+        nc.scalar.activation(out=pairs[:, c, :], in_=raw01[:, :, c].rearrange("p j t -> p t j"), func=COPY)
+
+        pair_words = pairs[:].rearrange("p t j -> p (t j)").bitcast(U32)
+        for s in range(SLICES):
+            picked_words = picked[s][:].rearrange("p n j -> p (n j)").bitcast(U32)
+            nc.vector.tensor_copy(out=picked_words[:, 0 : 2 * SLICE : 2], in_=pair_words.indirect(listed(s)))
+
+        for c in spans(ROW3_CUTS):
+            nc.scalar.activation(out=row3[:, c], in_=raw3[:, c], func=COPY)
+        for s in range(SLICES):
+            nc.scalar.activation(out=picked[s][:, :, 3], in_=row3[:].indirect(listed(s)), func=COPY)
+
+        def quantize_x(s):
+            nc.vector.quantize_mx(
+                out=x_codes[:, s * SLICE : (s + 1) * SLICE].bitcast(FP8X4),
+                scales=x_scales[:, s * SLICE : (s + 1) * SLICE],
+                in_=picked[s][:].rearrange("p n j -> p (n j)"),
+            )
+
+        def quantize_w(h):
+            nc.vector.quantize_mx(
+                out=w_codes[h][:].bitcast(FP8X4),
+                scales=w_scales[h][:],
+                in_=w_bf[h][:].rearrange("p m j -> p (m j)"),
+            )
+
+        def multiply(acc, t, entries):
+            cols = slice((t % 2) * P, (t % 2 + 1) * P)
+            nc.tensor.matmul_mx(
+                out=acc,
+                lhsT=w_codes[t // 2][:, cols].bitcast(FP8X4),
+                lhsT_scale=w_scales[t // 2][:, cols],
+                rhs=x_codes[:, entries].bitcast(FP8X4),
+                rhs_scale=x_scales[:, entries],
+                start=True,
+                stop=True,
+            )
+
+        def multiply_low(s):
+            for t in range(2):
+                multiply(banks[s][:, t * SLICE : (t + 1) * SLICE], t, slice(s * SLICE, (s + 1) * SLICE))
+
+        def take_max(dst, src):
+            nc.vector.tensor_reduce(out=dst, in_=src, axis=mybir.AxisListType.X, op=mybir.AluOpType.max)
+
+        def max_low(s):
+            centres = slice(s * (SLICE // D), (s + 1) * (SLICE // D))
+            take_max(pooled01[:, :, centres], banks[s][:].rearrange("p (t v d) -> p t v d", t=2, d=D))
+
+        def add_bias(dst, src, t):
+            nc.scalar.activation(out=dst, in_=src, func=IDENTITY, bias=bias[:, t : t + 1])
+
+        nc.vector.tensor_copy(out=w_bf[0][:], in_=w_raw[0][:].rearrange("p j m -> p m j"))
+        quantize_x(0)
+        quantize_w(0)
+        multiply_low(0)
+        quantize_x(1)
+        multiply_low(1)
+        quantize_x(2)
+        multiply_low(2)
+        nc.scalar.activation(out=w_bf[1][:], in_=w_raw[1][:].rearrange("p j m -> p m j"), func=COPY)
+        max_low(0)
+        quantize_x(3)
+        multiply_low(3)
+        max_low(1)
+        max_low(2)
+        quantize_w(1)
+        for t in (2, 3):
+            for u in range(2):
+                multiply(banks[2 * t + u][:], t, slice(u * 2 * SLICE, (u + 1) * 2 * SLICE))
+        max_low(3)
+        for u in range(2):
+            add_bias(biased3[:, u * 2 * SLICE : (u + 1) * 2 * SLICE], banks[6 + u][:], 3)
+        for u in range(2):
+            take_max(pooled2[:, u * (V // 2) : (u + 1) * (V // 2)], banks[4 + u][:].rearrange("p (v d) -> p v d", d=D))
+        for t in range(2):
+            add_bias(result01[:, t, :], pooled01[:, t, :], t)
+        nc.sync.dma_start(out=out[0 : 2 * P, :].rearrange("(t p) v -> p t v", p=P), in_=result01[:])
+        add_bias(result2[:], pooled2[:], 2)
+        nc.sync.dma_start(out=out[2 * P : 3 * P, :], in_=result2[:])
+        take_max(result3[:], biased3[:].rearrange("p (v d) -> p v d", d=D))
+        nc.sync.dma_start(out=out[3 * P : 4 * P, :], in_=result3[:])

@@ -45,7 +45,7 @@ def tile_picked_pool_lin_bias_sub_e_kernel(tc, xT, w, b, offs, out):
         pairs = keep.tile([P, T, 2], BF16, name="pairs")
         row2 = keep.tile([P, T], BF16, name="row2")
         row3 = keep.tile([P, T], BF16, name="row3")
-        picked = [keep.tile([P, SLICE, PACK], BF16, name="picked%d" % s, align_bytes=64) for s in range(SLICES)]
+        picked = keep.tile([P, S, PACK], BF16, name="picked", align_bytes=64)
         x_codes = keep.tile([P, S], U32, name="x_codes", align_bytes=64)
         x_scales = keep.tile([P, S], U8, name="x_scales", align_bytes=64)
         w_raw = [keep.tile([P, PACK, HALF], F32, name="w_raw%d" % h) for h in range(2)]
@@ -57,7 +57,8 @@ def tile_picked_pool_lin_bias_sub_e_kernel(tc, xT, w, b, offs, out):
         result01 = keep.tile([P, 2, V], F32, name="result01")
         pooled2 = keep.tile([P, V], F32, name="pooled2")
         result2 = keep.tile([P, V], F32, name="result2")
-        biased3 = keep.tile([P, S], F32, name="biased3")
+        biased3 = keep.tile([P, S // 2], F32, name="biased3")
+        pooled3 = keep.tile([P, V // 2], F32, name="pooled3")
         result3 = keep.tile([P, V], F32, name="result3")
         warm_in = keep.tile([P, 1], F32, name="warm_in")
         warm_out = keep.tile([P, 1], F32, name="warm_out")
@@ -84,8 +85,7 @@ def tile_picked_pool_lin_bias_sub_e_kernel(tc, xT, w, b, offs, out):
 
         for c in spans(ROW2_CUTS):
             nc.vector.tensor_copy(out=row2[:, c], in_=raw2[:, c])
-        for s in range(SLICES):
-            nc.scalar.activation(out=picked[s][:, :, 2], in_=row2[:].indirect(listed(s)), func=COPY)
+        nc.scalar.activation(out=picked[:, :, 2], in_=row2[:].indirect(offsets[:]), func=COPY)
 
         for c in spans(PAIR_CUTS[:-1] + [PAIR_LAST_SPLIT]):
             nc.vector.tensor_copy(out=pairs[:, c, :], in_=raw01[:, :, c].rearrange("p j t -> p t j"))
@@ -93,27 +93,27 @@ def tile_picked_pool_lin_bias_sub_e_kernel(tc, xT, w, b, offs, out):
         nc.scalar.activation(out=pairs[:, c, :], in_=raw01[:, :, c].rearrange("p j t -> p t j"), func=COPY)
 
         pair_words = pairs[:].rearrange("p t j -> p (t j)").bitcast(U32)
-        for s in range(SLICES):
-            picked_words = picked[s][:].rearrange("p n j -> p (n j)").bitcast(U32)
-            nc.vector.tensor_copy(out=picked_words[:, 0 : 2 * SLICE : 2], in_=pair_words.indirect(listed(s)))
+        picked_words = picked[:].rearrange("p n j -> p (n j)").bitcast(U32)
+        nc.vector.tensor_copy(out=picked_words[:, 0 : 2 * S : 2], in_=pair_words.indirect(offsets[:]))
 
         for c in spans(ROW3_CUTS):
             nc.scalar.activation(out=row3[:, c], in_=raw3[:, c], func=COPY)
-        for s in range(SLICES):
-            nc.scalar.activation(out=picked[s][:, :, 3], in_=row3[:].indirect(listed(s)), func=COPY)
+
+        def gather_row3(s):
+            nc.scalar.activation(out=picked[:, s * SLICE : (s + 1) * SLICE, 3], in_=row3[:].indirect(listed(s)), func=COPY)
 
         def quantize_x(s):
             nc.vector.quantize_mx(
                 out=x_codes[:, s * SLICE : (s + 1) * SLICE].bitcast(FP8X4),
                 scales=x_scales[:, s * SLICE : (s + 1) * SLICE],
-                in_=picked[s][:].rearrange("p n j -> p (n j)"),
+                in_=picked[:, s * SLICE : (s + 1) * SLICE, :].rearrange("p n j -> p (n j)"),
             )
 
-        def quantize_w(h):
+        def quantize_w(h, cols):
             nc.vector.quantize_mx(
-                out=w_codes[h][:].bitcast(FP8X4),
-                scales=w_scales[h][:],
-                in_=w_bf[h][:].rearrange("p m j -> p (m j)"),
+                out=w_codes[h][:, cols].bitcast(FP8X4),
+                scales=w_scales[h][:, cols],
+                in_=w_bf[h][:, cols, :].rearrange("p m j -> p (m j)"),
             )
 
         def multiply(acc, t, entries):
@@ -142,33 +142,46 @@ def tile_picked_pool_lin_bias_sub_e_kernel(tc, xT, w, b, offs, out):
         def add_bias(dst, src, t):
             nc.scalar.activation(out=dst, in_=src, func=IDENTITY, bias=bias[:, t : t + 1])
 
+        def multiply_high(t, u):
+            multiply(banks[2 * t + u][:], t, slice(u * 2 * SLICE, (u + 1) * 2 * SLICE))
+
+        def grouped(ap):
+            return ap.rearrange("p (v d) -> p v d", d=D)
+
+        lower, upper = slice(0, P), slice(P, 2 * P)
+        for s in range(SLICES):
+            gather_row3(s)
+        nc.scalar.activation(out=w_bf[1][:, upper, :], in_=w_raw[1][:, :, upper].rearrange("p j m -> p m j"), func=COPY)
         nc.vector.tensor_copy(out=w_bf[0][:], in_=w_raw[0][:].rearrange("p j m -> p m j"))
         quantize_x(0)
-        quantize_w(0)
+        quantize_w(0, slice(0, HALF))
         multiply_low(0)
+        nc.vector.tensor_copy(out=w_bf[1][:, lower, :], in_=w_raw[1][:, :, lower].rearrange("p j m -> p m j"))
         quantize_x(1)
         multiply_low(1)
+        quantize_w(1, lower)
+        multiply_high(2, 0)
+        max_low(0)
         quantize_x(2)
         multiply_low(2)
-        nc.scalar.activation(out=w_bf[1][:], in_=w_raw[1][:].rearrange("p j m -> p m j"), func=COPY)
-        max_low(0)
+        max_low(1)
         quantize_x(3)
         multiply_low(3)
-        max_low(1)
+        take_max(pooled2[:, 0 : V // 2], grouped(banks[4][:]))
+        quantize_w(1, upper)
+        multiply_high(2, 1)
+        multiply_high(3, 1)
+        add_bias(biased3[:], banks[7][:], 3)
+        multiply_high(3, 0)
         max_low(2)
-        quantize_w(1)
-        for t in (2, 3):
-            for u in range(2):
-                multiply(banks[2 * t + u][:], t, slice(u * 2 * SLICE, (u + 1) * 2 * SLICE))
         max_low(3)
-        for u in range(2):
-            add_bias(biased3[:, u * 2 * SLICE : (u + 1) * 2 * SLICE], banks[6 + u][:], 3)
-        for u in range(2):
-            take_max(pooled2[:, u * (V // 2) : (u + 1) * (V // 2)], banks[4 + u][:].rearrange("p (v d) -> p v d", d=D))
         for t in range(2):
             add_bias(result01[:, t, :], pooled01[:, t, :], t)
         nc.sync.dma_start(out=out[0 : 2 * P, :].rearrange("(t p) v -> p t v", p=P), in_=result01[:])
+        take_max(pooled2[:, V // 2 : V], grouped(banks[5][:]))
         add_bias(result2[:], pooled2[:], 2)
         nc.sync.dma_start(out=out[2 * P : 3 * P, :], in_=result2[:])
-        take_max(result3[:], biased3[:].rearrange("p (v d) -> p v d", d=D))
+        take_max(pooled3[:], grouped(banks[6][:]))
+        add_bias(result3[:, 0 : V // 2], pooled3[:], 3)
+        take_max(result3[:, V // 2 : V], grouped(biased3[:]))
         nc.sync.dma_start(out=out[3 * P : 4 * P, :], in_=result3[:])

@@ -152,9 +152,11 @@ def tile_picked_pool_lin_bias_sub_e_kernel(tc, xT, w, b, offs, out):
         for s in range(SLICES):
             gather_row3(s)
         nc.scalar.activation(out=w_bf[1][:, upper, :], in_=w_raw[1][:, :, upper].rearrange("p j m -> p m j"), func=COPY)
-        nc.vector.tensor_copy(out=w_bf[0][:], in_=w_raw[0][:].rearrange("p j m -> p m j"))
+        for c in (lower, upper):
+            nc.vector.tensor_copy(out=w_bf[0][:, c, :], in_=w_raw[0][:, :, c].rearrange("p j m -> p m j"))
         quantize_x(0)
-        quantize_w(0, slice(0, HALF))
+        for c in (lower, upper):
+            quantize_w(0, c)
         multiply_low(0)
         nc.vector.tensor_copy(out=w_bf[1][:, lower, :], in_=w_raw[1][:, :, lower].rearrange("p j m -> p m j"))
         quantize_x(1)

from contextlib import ExitStack

import concourse.mybir as mybir

K, T, D, S, V, N = 512, 2048, 16, 1024, 64, 512
FLOPS = 2 * K * N * S

F32 = mybir.dt.float32
BF16 = mybir.dt.bfloat16
U32 = mybir.dt.uint32
U16 = mybir.dt.uint16
U8 = mybir.dt.uint8
FP8X4 = mybir.dt.float8_e4m3fn_x4
COPY = mybir.ActivationFunctionType.Copy
IDENTITY = mybir.ActivationFunctionType.Identity

P = 128
PACK = 4
SLICE = 256
SLICES = S // SLICE
HALF = 256
ROW2_CUTS = [0, 1024, 2048]
PAIR_CUTS = [0, 1024, 1536, 2048]
PAIR_LAST_SPLIT = 1856
ROW3_CUTS = [0, 512, 1024, 1536, 2048]


def spans(cuts):
    return [slice(a, c) for a, c in zip(cuts[:-1], cuts[1:])]


def tile_picked_pool_lin_bias_sub_e_kernel(tc, xT, w, b, offs, out):
    nc = tc.nc
    xv = xT.rearrange("(p j) t -> p j t", j=PACK)
    wv = w.rearrange("(p j) m -> p j m", j=PACK)

    with ExitStack() as ctx:
        keep = ctx.enter_context(tc.tile_pool(name="keep", bufs=1))
        psum = ctx.enter_context(tc.psum_pool(name="psum", bufs=1))

        offsets = keep.tile([P, S // 16], U16, name="offsets")
        raw01 = keep.tile([P, 2, T], F32, name="raw01")
        raw2 = keep.tile([P, T], F32, name="raw2")
        raw3 = keep.tile([P, T], F32, name="raw3")
        pairs = keep.tile([P, T, 2], BF16, name="pairs")
        row2 = keep.tile([P, T], BF16, name="row2")
        row3 = keep.tile([P, T], BF16, name="row3")
        picked = keep.tile([P, S, PACK], BF16, name="picked", align_bytes=64)
        x_codes = keep.tile([P, S], U32, name="x_codes", align_bytes=64)
        x_scales = keep.tile([P, S], U8, name="x_scales", align_bytes=64)
        w_raw = [keep.tile([P, PACK, HALF], F32, name="w_raw%d" % h) for h in range(2)]
        w_bf = [keep.tile([P, HALF, PACK], BF16, name="w_bf%d" % h, align_bytes=64) for h in range(2)]
        w_codes = [keep.tile([P, HALF], U32, name="w_codes%d" % h, align_bytes=64) for h in range(2)]
        w_scales = [keep.tile([P, HALF], U8, name="w_scales%d" % h, align_bytes=64) for h in range(2)]
        bias = keep.tile([P, N // P], F32, name="bias")
        pooled01 = keep.tile([P, 2, V], F32, name="pooled01")
        result01 = keep.tile([P, 2, V], F32, name="result01")
        pooled2 = keep.tile([P, V], F32, name="pooled2")
        result2 = keep.tile([P, V], F32, name="result2")
        biased3 = keep.tile([P, S // 2], F32, name="biased3")
        pooled3 = keep.tile([P, V // 2], F32, name="pooled3")
        result3 = keep.tile([P, V], F32, name="result3")
        warm_in = keep.tile([P, 1], F32, name="warm_in")
        warm_out = keep.tile([P, 1], F32, name="warm_out")
        banks = [psum.tile([P, 2 * SLICE], F32, name="bank%d" % i) for i in range(8)]

        def listed(s):
            return offsets[:, s * (SLICE // 16) : (s + 1) * (SLICE // 16)]

        nc.gpsimd.memset(warm_in[:], 0.0)
        nc.scalar.activation(out=warm_out[:], in_=warm_in[:], func=COPY)

        first, second = spans(ROW2_CUTS)
        nc.sync.dma_start(out=raw2[:, first], in_=xv[:, 2, first])
        nc.sync.dma_start(offsets[:], offs)
        nc.sync.dma_start(out=raw2[:, second], in_=xv[:, 2, second])
        for c in spans(PAIR_CUTS):
            nc.sync.dma_start(out=raw01[:, :, c], in_=xv[:, 0:2, c])
        for c in spans(ROW3_CUTS):
            nc.sync.dma_start(out=raw3[:, c], in_=xv[:, 3, c])
        for h in range(2):
            nc.sync.dma_start(out=w_raw[h][:], in_=wv[:, :, h * HALF : (h + 1) * HALF])
        with nc.allow_non_contiguous_dma(reason="one bias value a partition"):
            nc.sync.dma_start(out=bias[:], in_=b.rearrange("(t p) o -> p (t o)", p=P))

        for c in spans(ROW2_CUTS):
            nc.vector.tensor_copy(out=row2[:, c], in_=raw2[:, c])
        nc.scalar.activation(out=picked[:, :, 2], in_=row2[:].indirect(offsets[:]), func=COPY)

        for c in spans(PAIR_CUTS[:-1] + [PAIR_LAST_SPLIT]):
            nc.vector.tensor_copy(out=pairs[:, c, :], in_=raw01[:, :, c].rearrange("p j t -> p t j"))
        c = slice(PAIR_LAST_SPLIT, T)
        nc.scalar.activation(out=pairs[:, c, :], in_=raw01[:, :, c].rearrange("p j t -> p t j"), func=COPY)

        pair_words = pairs[:].rearrange("p t j -> p (t j)").bitcast(U32)
        picked_words = picked[:].rearrange("p n j -> p (n j)").bitcast(U32)
        nc.vector.tensor_copy(out=picked_words[:, 0 : 2 * S : 2], in_=pair_words.indirect(offsets[:]))

        for c in spans(ROW3_CUTS):
            nc.scalar.activation(out=row3[:, c], in_=raw3[:, c], func=COPY)

        def gather_row3(s):
            nc.scalar.activation(out=picked[:, s * SLICE : (s + 1) * SLICE, 3], in_=row3[:].indirect(listed(s)), func=COPY)

        def quantize_x(s):
            nc.vector.quantize_mx(
                out=x_codes[:, s * SLICE : (s + 1) * SLICE].bitcast(FP8X4),
                scales=x_scales[:, s * SLICE : (s + 1) * SLICE],
                in_=picked[:, s * SLICE : (s + 1) * SLICE, :].rearrange("p n j -> p (n j)"),
            )

        def quantize_w(h, cols):
            nc.vector.quantize_mx(
                out=w_codes[h][:, cols].bitcast(FP8X4),
                scales=w_scales[h][:, cols],
                in_=w_bf[h][:, cols, :].rearrange("p m j -> p (m j)"),
            )

        def multiply(acc, t, entries):
            cols = slice((t % 2) * P, (t % 2 + 1) * P)
            nc.tensor.matmul_mx(
                out=acc,
                lhsT=w_codes[t // 2][:, cols].bitcast(FP8X4),
                lhsT_scale=w_scales[t // 2][:, cols],
                rhs=x_codes[:, entries].bitcast(FP8X4),
                rhs_scale=x_scales[:, entries],
                start=True,
                stop=True,
            )

        def multiply_low(s):
            for t in range(2):
                multiply(banks[s][:, t * SLICE : (t + 1) * SLICE], t, slice(s * SLICE, (s + 1) * SLICE))

        def take_max(dst, src):
            nc.vector.tensor_reduce(out=dst, in_=src, axis=mybir.AxisListType.X, op=mybir.AluOpType.max)

        def max_low(s):
            centres = slice(s * (SLICE // D), (s + 1) * (SLICE // D))
            take_max(pooled01[:, :, centres], banks[s][:].rearrange("p (t v d) -> p t v d", t=2, d=D))

        def add_bias(dst, src, t):
            nc.scalar.activation(out=dst, in_=src, func=IDENTITY, bias=bias[:, t : t + 1])

        def multiply_high(t, u):
            multiply(banks[2 * t + u][:], t, slice(u * 2 * SLICE, (u + 1) * 2 * SLICE))

        def grouped(ap):
            return ap.rearrange("p (v d) -> p v d", d=D)

        lower, upper = slice(0, P), slice(P, 2 * P)
        for s in range(SLICES):
            gather_row3(s)
        nc.scalar.activation(out=w_bf[1][:, upper, :], in_=w_raw[1][:, :, upper].rearrange("p j m -> p m j"), func=COPY)
        for c in (lower, upper):
            nc.vector.tensor_copy(out=w_bf[0][:, c, :], in_=w_raw[0][:, :, c].rearrange("p j m -> p m j"))
        quantize_x(0)
        for c in (lower, upper):
            quantize_w(0, c)
        multiply_low(0)
        nc.vector.tensor_copy(out=w_bf[1][:, lower, :], in_=w_raw[1][:, :, lower].rearrange("p j m -> p m j"))
        quantize_x(1)
        multiply_low(1)
        quantize_w(1, lower)
        multiply_high(2, 0)
        max_low(0)
        quantize_x(2)
        multiply_low(2)
        max_low(1)
        quantize_x(3)
        multiply_low(3)
        take_max(pooled2[:, 0 : V // 2], grouped(banks[4][:]))
        quantize_w(1, upper)
        multiply_high(2, 1)
        multiply_high(3, 1)
        add_bias(biased3[:], banks[7][:], 3)
        multiply_high(3, 0)
        max_low(2)
        max_low(3)
        for t in range(2):
            add_bias(result01[:, t, :], pooled01[:, t, :], t)
        nc.sync.dma_start(out=out[0 : 2 * P, :].rearrange("(t p) v -> p t v", p=P), in_=result01[:])
        take_max(pooled2[:, V // 2 : V], grouped(banks[5][:]))
        add_bias(result2[:], pooled2[:], 2)
        nc.sync.dma_start(out=out[2 * P : 3 * P, :], in_=result2[:])
        take_max(pooled3[:], grouped(banks[6][:]))
        add_bias(result3[:, 0 : V // 2], pooled3[:], 3)
        take_max(result3[:, V // 2 : V], grouped(biased3[:]))
        nc.sync.dma_start(out=out[3 * P : 4 * P, :], in_=result3[:])
